import numpy as np
import ml_dtypes


def mxq(x, axis, fmt="e4m3"):
    dtype, down = {"e4m3": (ml_dtypes.float8_e4m3fn, 7), "e5m2": (ml_dtypes.float8_e5m2, 14)}[fmt]
    v = np.moveaxis(np.asarray(x, np.float32).astype(ml_dtypes.bfloat16).astype(np.float64), axis, -1)
    blocks = v.reshape(v.shape[:-1] + (-1, 32))
    amax = np.abs(blocks).max(-1, keepdims=True)
    byte = np.maximum(np.where(amax > 0, np.frexp(amax)[1] - 1 + 127, 0) - down, 1)
    scale = np.exp2(byte - 127.0)
    codes = (blocks / scale).astype(np.float32).astype(dtype).astype(np.float64)
    return np.moveaxis((codes * scale).reshape(v.shape), -1, axis)


WIDE = False


def mx_kscale(k):
    if not WIDE:
        return np.ones(k)
    levels = np.array([10, -10, 5, -5, 0])
    if k % 512:
        return np.exp2(np.random.permutation(np.resize(levels, k // 32))).repeat(32)
    a = np.empty((k // 512, 16))
    for p in range(k // 512):
        a[p, :8] = np.random.permutation(np.resize(levels, 8))
        for g in range(8):
            far = levels[np.abs(levels - a[p, g]) >= 10]
            a[p, g + 8] = far[np.random.randint(len(far))]
    return np.exp2(a.ravel()).repeat(32)


def f64(x):
    return np.asarray(x).astype(np.float64)


def striped(idx):
    return np.tile(idx.reshape(-1, 16).T, (8, 1)).astype(np.uint16)


def unstriped(offs):
    return offs[:16].T.reshape(-1).astype(np.int64)


E2M1 = np.array([0.0, 0.5, 1.0, 1.5, 2.0, 3.0, 4.0, 6.0, -0.0, -0.5, -1.0, -1.5, -2.0, -3.0, -4.0, -6.0])


def pack_weight(w, fmt):
    k, n = w.shape
    w = f64(np.asarray(w, np.float32).astype(ml_dtypes.bfloat16)).reshape(k // 32, 32, n)
    amax = np.abs(w).max(1)
    if fmt == "e4m3":
        byte = np.frexp(amax)[1] - 1 + 127 - 7
    else:
        mant, ex = np.frexp(amax / 6.0)
        byte = np.where(mant > 0.5, ex, ex - 1) + 127
    byte = np.clip(np.where(amax > 0, byte, 1), 1, 254)
    scaled = (w * np.exp2(127.0 - byte)[:, None, :]).reshape(k, n).astype(np.float32)
    by_word = np.ascontiguousarray(scaled.reshape(k // 512, 128, 4, n).transpose(0, 1, 3, 2))
    if fmt == "e4m3":
        words = by_word.astype(ml_dtypes.float8_e4m3fn).view(np.uint8)
    else:
        c = by_word.astype(ml_dtypes.float4_e2m1fn).view(np.uint8) & 0xF
        words = (c[..., 0::2] | (c[..., 1::2] << 4)).reshape(k // 512, 128, 2 * n)
    return np.ascontiguousarray(words), np.ascontiguousarray(byte.astype(np.uint8).reshape(k // 512, 16, n))


def unpack_weight(words, scales, fmt):
    g, _, n = scales.shape
    words = np.ascontiguousarray(words).reshape(g, 128, n, -1)
    if fmt == "e4m3":
        vals = words.view(ml_dtypes.float8_e4m3fn).astype(np.float64)
    else:
        nib = np.empty((g, 128, n, 4), np.uint8)
        nib[..., 0::2] = words & 0xF
        nib[..., 1::2] = words >> 4
        vals = E2M1[nib]
    vals = vals * np.repeat(np.exp2(scales.astype(np.float64) - 127.0), 8, axis=1)[..., None]
    return vals.transpose(0, 1, 3, 2).reshape(g * 512, n)


K, T, E, C, H, N, TOP = 256, 512, 8, 256, 512, 1024, 4


def by_expert(wq, xq):
    return np.concatenate([wq[e].T @ xq[:, e * C:(e + 1) * C] for e in range(E)], axis=1)


def setup_inputs():
    n = np.random.standard_normal
    v = mx_kscale(N)
    u = mx_kscale(H)
    deal = np.repeat(np.arange(E), C).reshape(TOP, T)[:, np.random.permutation(T)]
    deal = np.take_along_axis(deal, np.argsort(np.random.rand(TOP, T), axis=0), axis=0)
    for _ in range(8):
        s_, t_ = np.random.permutation(T).reshape(2, -1); r = np.random.randint(TOP, size=T // 2); x, y = deal[r, s_].copy(), deal[r, t_].copy()
        ok = ~((deal[:, s_] == y).any(0) | (deal[:, t_] == x).any(0)); deal[r[ok], s_[ok]] = y[ok]; deal[r[ok], t_[ok]] = x[ok]
    order = np.lexsort((np.random.rand(TOP * T), deal.reshape(-1)))
    slot_token = order % T; pos = np.empty(TOP * T, np.int64); pos[order] = np.arange(TOP * T); pos = pos.reshape(TOP, T)
    g = np.random.uniform(0.5, 1.5, (TOP, T)); g = g / g.sum(0)
    w_slot = np.empty(E * C)
    for r in range(TOP): w_slot[pos[r]] = g[r]
    dy = pack_weight(n((N, T)) * v[:, None], "e4m3")
    wt = pack_weight(n((N, K)) / np.sqrt(N) / v[:, None], "e4m3")
    return {
        "dy_words": dy[0],
        "dy_scales": dy[1],
        "wt_words": wt[0],
        "wt_scales": wt[1],
        "wbt": (n((E, N, H)) / np.sqrt(N) / v[None, :, None] * u).astype(np.float32),
        "wat": (n((E, H, K)) / np.sqrt(H) / u[None, :, None]).astype(np.float32),
        "gate": (np.tile(w_slot, (128, 1))).astype(np.float32),
        "offs": striped(slot_token),
        "pos1": striped(pos[0]),
        "pos2": striped(pos[1]),
        "pos3": striped(pos[2]),
        "pos4": striped(pos[3]),
    }


def reference(dy_words, dy_scales, wt_words, wt_scales, wbt, wat, gate, offs, pos1, pos2, pos3, pos4):
    wt = unpack_weight(wt_words, wt_scales, "e4m3")
    wbtq = mxq(f64(wbt), 1, "e4m3")
    watq = mxq(f64(wat), 1, "e4m3")
    idx = unstriped(offs)
    dy = unpack_weight(dy_words, dy_scales, "e4m3")
    base = wt.T @ dy
    dh = f64(gate[:1]) * by_expert(wbtq, dy[:, idx])
    dx = by_expert(watq, mxq(dh, 0, "e4m3"))
    c = dx[:, unstriped(pos1)] + dx[:, unstriped(pos2)] + dx[:, unstriped(pos3)] + dx[:, unstriped(pos4)]
    return base + c

@@ -1,0 +1,273 @@
+from contextlib import ExitStack
+
+import concourse.mybir as mybir
+
+K, T, E, C, H, N, TOP = 256, 512, 8, 256, 512, 1024, 4
+FLOPS = 2 * N * K * T + 2 * E * C * H * (N + K)
+
+F32 = mybir.dt.float32
+BF16 = mybir.dt.bfloat16
+I32 = mybir.dt.int32
+U32 = mybir.dt.uint32
+U16 = mybir.dt.uint16
+U8 = mybir.dt.uint8
+FP8X4 = mybir.dt.float8_e4m3fn_x4
+ADD = mybir.AluOpType.add
+MULT = mybir.AluOpType.mult
+
+P = 128
+PACK = 4
+PASSES = N // (P * PACK)
+KB = K // P
+SLOTS = E * C
+WAT_LAG = 2
+GATHER_LEAD = 4
+RAW_SLOTS = 12
+RAW_BYTES = PACK * H * 4
+
+
+def tile_moe_adb_none_kernel(
+    tc, dy_words, dy_scales, wt_words, wt_scales, wbt, wat, gate, offs, pos1, pos2, pos3, pos4, out
+):
+    nc = tc.nc
+    with ExitStack() as ctx:
+        keep = ctx.enter_context(tc.tile_pool(name="keep", bufs=1))
+        raw_b = ctx.enter_context(tc.tile_pool(name="raw_b", bufs=1))
+        half_b = ctx.enter_context(tc.tile_pool(name="half_b", bufs=3))
+        ring = ctx.enter_context(tc.tile_pool(name="ring", bufs=3))
+        code_b = ctx.enter_context(tc.tile_pool(name="code_b", bufs=3))
+        ps_h = ctx.enter_context(tc.psum_pool(name="ps_h", bufs=4))
+        ps_x = ctx.enter_context(tc.psum_pool(name="ps_x", bufs=2))
+        ps_b = ctx.enter_context(tc.psum_pool(name="ps_b", bufs=2))
+
+        offs_sb = keep.tile([P, SLOTS // 16], U16, name="offs_sb")
+        pos_sb = [keep.tile([P, T // 16], U16, name="pos_sb%d" % r) for r in range(TOP)]
+        dyw = [keep.tile([P, T], I32, name="dyw%d" % s, align_bytes=64) for s in range(PASSES)]
+        dys = keep.tile([P, T], U8, name="dys", align_bytes=64)
+        wtw = keep.tile([P, PASSES, K], I32, name="wtw", align_bytes=64)
+        wts = keep.tile([P, K], U8, name="wts", align_bytes=64)
+        gate_sb = [keep.tile([P, SLOTS // 2], F32, name="gate_sb%d" % u) for u in range(2)]
+        dx = [keep.tile([P, SLOTS], F32, name="dx%d" % kb) for kb in range(KB)]
+
+        def load_words(dst, src):
+            nc.sync.dma_start(out=dst, in_=src.rearrange("p x d -> p (x d)").bitcast(I32))
+
+        def load_scales(plane, src):
+            nc.vector.memset(plane[:].bitcast(I32), 0)
+            for q in range(4):
+                nc.sync.dma_start(
+                    out=plane[32 * q : 32 * q + 4 * PASSES, :].bitcast(I32),
+                    in_=src[:, 4 * q : 4 * q + 4, :].bitcast(I32),
+                )
+
+        def raw_offset(e, s):
+            chunk = PASSES * e + s
+            return (chunk if chunk < RAW_SLOTS else PASSES * (chunk - RAW_SLOTS)) * RAW_BYTES
+
+        def wat_offset(e):
+            return RAW_SLOTS * RAW_BYTES + e % 4 * PACK * K * 4
+
+        def held(shape, dtype, name, e, s, at):
+            if 0 <= e < E:
+                return raw_b.tile(shape, dtype, name=name, offset=raw_offset(e, s) + at, align_bytes=64)
+            return keep.tile(shape, dtype, name=name, align_bytes=64)
+
+        def load_wbt(e, s):
+            raw = raw_b.tile([P, PACK, H], F32, name="raw%d_%d" % (e, s), offset=raw_offset(e, s), align_bytes=64)
+            nc.sync.dma_start(out=raw[:], in_=wbt[e, s * 512 : (s + 1) * 512, :].rearrange("(p j) i -> p j i", j=PACK))
+            return raw
+
+        def load_wat(e):
+            raw = raw_b.tile([P, PACK, K], F32, name="raw_a%d" % e, offset=wat_offset(e), align_bytes=64)
+            nc.sync.dma_start(out=raw[:], in_=wat[e].rearrange("(p j) k -> p j k", j=PACK))
+            return raw
+
+        def cast_wbt(raw, half, split):
+            dst = half.rearrange("p (t m j) -> p m j t", t=PACK, j=PACK)
+            src = raw[:].rearrange("p j (m t) -> p m j t", t=PACK)
+            nc.scalar.copy(dst[:, :split], src[:, :split])
+            if split < P:
+                nc.vector.tensor_copy(dst[:, split:], src[:, split:])
+
+        def cast_wat(raw, half, copy):
+            copy(
+                half.rearrange("p (c i j) -> p c j i", i=4, j=PACK),
+                raw[:].rearrange("p j (c i) -> p c j i", i=4),
+            )
+
+        def quantize(mx, half, c0, c1):
+            codes, scales = mx
+            nc.vector.quantize_mx(
+                out=codes[:, c0:c1].bitcast(FP8X4), scales=scales[:, c0:c1], in_=half[:, c0 * PACK : c1 * PACK]
+            )
+
+        def cols_of(mx, c0, c1):
+            return mx[0][:, c0:c1].bitcast(FP8X4), mx[1][:, c0:c1]
+
+        def gather(e):
+            idx = offs_sb[:, e * C // 16 : (e + 1) * C // 16]
+            words = []
+            for s in range(PASSES):
+                w = held([P, C], U32, "gw%d_%d" % (e, s), e - GATHER_LEAD, 1, s * C * 4)
+                nc.vector.tensor_copy(w[:], dyw[s][:].bitcast(U32).indirect(idx))
+                words.append(w)
+            z = held([P, C], U8, "gs%d" % e, e - GATHER_LEAD, 1, PASSES * C * 4)
+            nc.vector.tensor_copy(z[:], dys[:].indirect(idx))
+            return words, z
+
+        def first_product(wq, g):
+            words, z = g
+            banks = []
+            for h in range(C // P):
+                cols = slice(h * P, (h + 1) * P)
+                bank = ps_h.tile([P, PACK, P], F32, name="bank")
+                for t in range(PACK):
+                    for s in range(PASSES):
+                        codes, scales = cols_of(wq, s * H + t * P, s * H + (t + 1) * P)
+                        nc.tensor.matmul_mx(
+                            out=bank[:, t, :],
+                            lhsT=codes,
+                            lhsT_scale=scales,
+                            rhs=words[s][:, cols].bitcast(FP8X4),
+                            rhs_scale=z[4 * s :, cols],
+                            start=(s == 0),
+                            stop=(s == PASSES - 1),
+                        )
+                banks.append(bank)
+            return banks
+
+        def apply_gate(e, banks, dh):
+            for h, bank in enumerate(banks):
+                u, j0 = divmod(e * C + h * P, SLOTS // 2)
+                nc.vector.tensor_tensor(
+                    dh[:, h * P * PACK : (h + 1) * P * PACK].rearrange("p (n t) -> p n t", t=PACK),
+                    bank[:].rearrange("p t n -> p n t"),
+                    gate_sb[u][:, j0 : j0 + P].unsqueeze(2).to_broadcast([P, P, PACK]),
+                    MULT,
+                )
+
+        def second_product(e, aq, hq):
+            bank = ps_x.tile([P, KB, C], F32, name="bank")
+            h_codes, h_scales = cols_of(hq, 0, C)
+            for kb in range(KB):
+                a_codes, a_scales = cols_of(aq, C + kb * P, C + (kb + 1) * P)
+                nc.tensor.matmul_mx(
+                    out=bank[:, kb, :],
+                    lhsT=a_codes,
+                    lhsT_scale=a_scales,
+                    rhs=h_codes,
+                    rhs_scale=h_scales,
+                    start=True,
+                    stop=True,
+                )
+            for kb in range(KB):
+                copy = nc.vector.tensor_copy if e < E - WAT_LAG else nc.scalar.copy
+                copy(dx[kb][:, e * C : (e + 1) * C], bank[:, kb, :])
+
+        def frozen_layer():
+            base = []
+            for kb in range(KB):
+                bank = ps_b.tile([P, T], F32, name="bank")
+                for s in range(PASSES):
+                    nc.tensor.matmul_mx(
+                        out=bank[:],
+                        lhsT=wtw[:, s, kb * P : (kb + 1) * P].bitcast(FP8X4),
+                        lhsT_scale=wts[4 * s :, kb * P : (kb + 1) * P],
+                        rhs=dyw[s][:].bitcast(FP8X4),
+                        rhs_scale=dys[4 * s :, :],
+                        start=(s == 0),
+                        stop=(s == PASSES - 1),
+                    )
+                base.append(bank)
+            return base
+
+        def leave_psum(banks):
+            base = []
+            for kb, bank in enumerate(banks):
+                part = raw_b.tile([P, T], F32, name="base%d" % kb, offset=wat_offset(E - 1) + kb * T * 4, align_bytes=64)
+                nc.scalar.copy(part[:], bank[:])
+                base.append(part)
+            return base
+
+        rb, ra, g, pair, pair_mx = {}, {}, {}, {}, {}
+
+        nc.sync.dma_start(offs_sb[:], offs)
+        load_words(dyw[0][:], dy_words[0])
+        load_words(dyw[1][:], dy_words[1])
+        load_scales(dys, dy_scales)
+        rb[0, 0] = load_wbt(0, 0)
+        rb[0, 1] = load_wbt(0, 1)
+        nc.sync.dma_start(gate_sb[0][:], gate[:, : SLOTS // 2])
+
+        for step in range(E + WAT_LAG):
+            e = step
+            if 0 < e < E:
+                rb[e, 0] = load_wbt(e, 0)
+                rb[e, 1] = load_wbt(e, 1)
+            if 0 <= e - WAT_LAG < E:
+                ra[e - WAT_LAG] = load_wat(e - WAT_LAG)
+            if e == 1:
+                for r, pos in enumerate((pos1, pos2, pos3, pos4)):
+                    nc.sync.dma_start(pos_sb[r][:], pos)
+            if e == 2:
+                load_scales(wts, wt_scales)
+            if e == 3:
+                nc.sync.dma_start(gate_sb[1][:], gate[:, SLOTS // 2 :])
+            if e == 4:
+                nc.sync.dma_start(out=wtw[:], in_=wt_words.rearrange("s p x d -> p s (x d)").bitcast(I32))
+            a = e - WAT_LAG
+            b = e - 1
+            last = e == E - 1
+            if e == 0:
+                for first in range(GATHER_LEAD):
+                    g[first] = gather(first)
+            if e < E:
+                half = half_b.tile([P, PASSES * H * PACK], BF16, name="half", align_bytes=64)
+                wq = (
+                    code_b.tile([P, PASSES * H], U32, name="wb_codes", align_bytes=64),
+                    code_b.tile([P, PASSES * H], U8, name="wb_scales", align_bytes=64),
+                )
+                cast_wbt(rb[e, 0], half[:, : H * PACK], P)
+                if last:
+                    quantize(wq, half, 0, H)
+                cast_wbt(rb[e, 1], half[:, H * PACK :], 48 if last else P)
+                quantize(wq, half, H if last else 0, PASSES * H)
+                if last:
+                    banks = first_product(wq, g[e])
+            if 0 <= b <= E:
+                pair_mx[b] = (
+                    held([P, C + K], U32, "pair_codes%d" % b, e, 1, 4096),
+                    held([P, C + K], U8, "pair_scales%d" % b, e, 1, 6144),
+                )
+                if a >= 0:
+                    cast_wat(ra[a], pair[b][:, C * PACK :], nc.scalar.copy)
+                if 0 < b < E - 1:
+                    quantize(pair_mx[b], pair[b], 0, C + K)
+                else:
+                    if a >= 0:
+                        quantize(pair_mx[b], pair[b], C, C + K)
+                    if b < E:
+                        quantize(pair_mx[b], pair[b], 0, C)
+                if a >= 0:
+                    second_product(a, pair_mx[b], pair_mx[a])
+            if e < E - 1:
+                banks = first_product(wq, g[e])
+            if e + GATHER_LEAD < E:
+                g[e + GATHER_LEAD] = gather(e + GATHER_LEAD)
+            if e <= E:
+                pair[e] = ring.tile([P, (C + K) * PACK], BF16, name="pair", align_bytes=64)
+            if e < E:
+                apply_gate(e, banks, pair[e])
+            if e == 4:
+                base_banks = frozen_layer()
+            if e == E + WAT_LAG - 1:
+                base = leave_psum(base_banks)
+
+        acc = base
+        for r in range(TOP):
+            for kb in range(KB):
+                nxt = keep.tile([P, T], F32, name="acc%d_%d" % (r, kb))
+                nc.vector.tensor_tensor(nxt[:], dx[kb][:].indirect(pos_sb[r][:]), acc[kb][:], ADD)
+                acc[kb] = nxt
+        for kb in range(KB):
+            nc.sync.dma_start(out=out[kb * P : (kb + 1) * P, :], in_=acc[kb][:])

@@ -20,7 +20,8 @@ PACK = 4
 PASSES = N // (P * PACK)
 KB = K // P
 SLOTS = E * C
-WAT_LAG = 2
+TAIL_WAT = 3
+SPLIT = 104
 GATHER_LEAD = 4
 RAW_SLOTS = 12
 RAW_BYTES = PACK * H * 4
@@ -146,7 +147,7 @@ def tile_moe_adb_none_kernel(
                     MULT,
                 )
 
-        def second_product(e, aq, hq):
+        def second_product(e, aq, hq, copy):
             bank = ps_x.tile([P, KB, C], F32, name="bank")
             h_codes, h_scales = cols_of(hq, 0, C)
             for kb in range(KB):
@@ -161,7 +162,6 @@ def tile_moe_adb_none_kernel(
                     stop=True,
                 )
             for kb in range(KB):
-                copy = nc.vector.tensor_copy if e < E - WAT_LAG else nc.scalar.copy
                 copy(dx[kb][:, e * C : (e + 1) * C], bank[:, kb, :])
 
         def frozen_layer():
@@ -181,13 +181,10 @@ def tile_moe_adb_none_kernel(
                 base.append(bank)
             return base
 
-        def leave_psum(banks):
-            base = []
-            for kb, bank in enumerate(banks):
-                part = raw_b.tile([P, T], F32, name="base%d" % kb, offset=wat_offset(E - 1) + kb * T * 4, align_bytes=64)
-                nc.scalar.copy(part[:], bank[:])
-                base.append(part)
-            return base
+        def leave_psum(kb, bank, e):
+            part = held([P, T], F32, "base%d" % kb, e, 0, 0)
+            nc.scalar.copy(part[:], bank[:])
+            return part
 
         rb, ra, g, pair, pair_mx = {}, {}, {}, {}, {}
 
@@ -199,69 +196,80 @@ def tile_moe_adb_none_kernel(
         rb[0, 1] = load_wbt(0, 1)
         nc.sync.dma_start(gate_sb[0][:], gate[:, : SLOTS // 2])
 
-        for step in range(E + WAT_LAG):
-            e = step
-            if 0 < e < E:
+        def new_pair_mx(b):
+            return (
+                held([P, C + K], U32, "pair_codes%d" % b, b + 1, 1, 4096),
+                held([P, C + K], U8, "pair_scales%d" % b, b + 1, 1, 6144),
+            )
+
+        base = []
+        for e in range(E):
+            last = e == E - 1
+            if e > 0:
                 rb[e, 0] = load_wbt(e, 0)
                 rb[e, 1] = load_wbt(e, 1)
-            if 0 <= e - WAT_LAG < E:
-                ra[e - WAT_LAG] = load_wat(e - WAT_LAG)
+            if 1 <= e <= E - TAIL_WAT:
+                ra[e - 1] = load_wat(e - 1)
+            if last:
+                for a in range(E - TAIL_WAT, E):
+                    ra[a] = load_wat(a)
             if e == 1:
                 for r, pos in enumerate((pos1, pos2, pos3, pos4)):
                     nc.sync.dma_start(pos_sb[r][:], pos)
             if e == 2:
                 load_scales(wts, wt_scales)
+                nc.sync.dma_start(out=wtw[:], in_=wt_words.rearrange("s p x d -> p s (x d)").bitcast(I32))
             if e == 3:
                 nc.sync.dma_start(gate_sb[1][:], gate[:, SLOTS // 2 :])
-            if e == 4:
-                nc.sync.dma_start(out=wtw[:], in_=wt_words.rearrange("s p x d -> p s (x d)").bitcast(I32))
-            a = e - WAT_LAG
-            b = e - 1
-            last = e == E - 1
             if e == 0:
                 for first in range(GATHER_LEAD):
                     g[first] = gather(first)
-            if e < E:
-                half = half_b.tile([P, PASSES * H * PACK], BF16, name="half", align_bytes=64)
-                wq = (
-                    code_b.tile([P, PASSES * H], U32, name="wb_codes", align_bytes=64),
-                    code_b.tile([P, PASSES * H], U8, name="wb_scales", align_bytes=64),
-                )
-                cast_wbt(rb[e, 0], half[:, : H * PACK], P)
-                if last:
-                    quantize(wq, half, 0, H)
-                cast_wbt(rb[e, 1], half[:, H * PACK :], 48 if last else P)
-                quantize(wq, half, H if last else 0, PASSES * H)
-                if last:
-                    banks = first_product(wq, g[e])
-            if 0 <= b <= E:
-                pair_mx[b] = (
-                    held([P, C + K], U32, "pair_codes%d" % b, e, 1, 4096),
-                    held([P, C + K], U8, "pair_scales%d" % b, e, 1, 6144),
-                )
-                if a >= 0:
-                    cast_wat(ra[a], pair[b][:, C * PACK :], nc.scalar.copy)
-                if 0 < b < E - 1:
-                    quantize(pair_mx[b], pair[b], 0, C + K)
-                else:
-                    if a >= 0:
-                        quantize(pair_mx[b], pair[b], C, C + K)
-                    if b < E:
-                        quantize(pair_mx[b], pair[b], 0, C)
-                if a >= 0:
-                    second_product(a, pair_mx[b], pair_mx[a])
-            if e < E - 1:
-                banks = first_product(wq, g[e])
-            if e + GATHER_LEAD < E:
-                g[e + GATHER_LEAD] = gather(e + GATHER_LEAD)
-            if e <= E:
+            half = half_b.tile([P, PASSES * H * PACK], BF16, name="half", align_bytes=64)
+            wq = (
+                code_b.tile([P, PASSES * H], U32, name="wb_codes", align_bytes=64),
+                code_b.tile([P, PASSES * H], U8, name="wb_scales", align_bytes=64),
+            )
+            cast_wbt(rb[e, 0], half[:, : H * PACK], SPLIT if last else P)
+            if last:
+                quantize(wq, half, 0, H)
+            cast_wbt(rb[e, 1], half[:, H * PACK :], 48 if last else SPLIT if e >= GATHER_LEAD else P)
+            quantize(wq, half, H if last else 0, PASSES * H)
+            if e in (5, 6):
+                base.append(leave_psum(e - 5, base_banks[e - 5], e))
+            if e >= GATHER_LEAD:
+                pair[e] = held([P, (C + K) * PACK], BF16, "pair%d" % e, e, 1, 0)
+            else:
                 pair[e] = ring.tile([P, (C + K) * PACK], BF16, name="pair", align_bytes=64)
-            if e < E:
+            b = e - 1
+            if last:
+                banks = first_product(wq, g[e])
                 apply_gate(e, banks, pair[e])
-            if e == 4:
+                pair[E] = ring.tile([P, (C + K) * PACK], BF16, name="pair", align_bytes=64)
+                for a in range(E - TAIL_WAT, E):
+                    cast_wat(ra[a], pair[a + 1][:, C * PACK :], nc.scalar.copy)
+            if b >= 0:
+                pair_mx[b] = new_pair_mx(b)
+                quantize(pair_mx[b], pair[b], 0, C + K if b > 0 else C)
+            if b >= 1:
+                second_product(b - 1, pair_mx[b], pair_mx[b - 1], nc.vector.tensor_copy if not last else nc.scalar.copy)
+            if not last:
+                banks = first_product(wq, g[e])
+                if e + GATHER_LEAD < E:
+                    g[e + GATHER_LEAD] = gather(e + GATHER_LEAD)
+                if 1 <= e <= E - TAIL_WAT:
+                    copy = nc.vector.tensor_copy if e >= GATHER_LEAD else nc.scalar.copy
+                    cast_wat(ra[e - 1], pair[e][:, C * PACK :], copy)
+                apply_gate(e, banks, pair[e])
+            if e == 2:
                 base_banks = frozen_layer()
-            if e == E + WAT_LAG - 1:
-                base = leave_psum(base_banks)
+
+        pair_mx[E - 1] = new_pair_mx(E - 1)
+        pair_mx[E] = new_pair_mx(E)
+        quantize(pair_mx[E - 1], pair[E - 1], 0, C)
+        quantize(pair_mx[E - 1], pair[E - 1], C, C + K)
+        quantize(pair_mx[E], pair[E], C, C + K)
+        second_product(E - 2, pair_mx[E - 1], pair_mx[E - 2], nc.vector.tensor_copy)
+        second_product(E - 1, pair_mx[E], pair_mx[E - 1], nc.scalar.copy)
 
         acc = base
         for r in range(TOP):

@@ -20,11 +20,13 @@ PACK = 4
 PASSES = N // (P * PACK)
 KB = K // P
 SLOTS = E * C
-TAIL_WAT = 3
-SPLIT = 104
+TAIL_WAT = 2
+HALF_SLOTS = 3
+LATE = (2, 2, 3, 3, 2, 0, 0, 0)
 GATHER_LEAD = 4
 RAW_SLOTS = 12
 RAW_BYTES = PACK * H * 4
+HALF_AT = RAW_SLOTS * RAW_BYTES + 4 * PACK * K * 4
 
 
 def tile_moe_adb_none_kernel(
@@ -34,8 +36,6 @@ def tile_moe_adb_none_kernel(
     with ExitStack() as ctx:
         keep = ctx.enter_context(tc.tile_pool(name="keep", bufs=1))
         raw_b = ctx.enter_context(tc.tile_pool(name="raw_b", bufs=1))
-        half_b = ctx.enter_context(tc.tile_pool(name="half_b", bufs=3))
-        ring = ctx.enter_context(tc.tile_pool(name="ring", bufs=3))
         code_b = ctx.enter_context(tc.tile_pool(name="code_b", bufs=3))
         ps_h = ctx.enter_context(tc.psum_pool(name="ps_h", bufs=4))
         ps_x = ctx.enter_context(tc.psum_pool(name="ps_x", bufs=2))
@@ -75,7 +75,12 @@ def tile_moe_adb_none_kernel(
 
         def load_wbt(e, s):
             raw = raw_b.tile([P, PACK, H], F32, name="raw%d_%d" % (e, s), offset=raw_offset(e, s), align_bytes=64)
-            nc.sync.dma_start(out=raw[:], in_=wbt[e, s * 512 : (s + 1) * 512, :].rearrange("(p j) i -> p j i", j=PACK))
+            rows = wbt[e, s * 512 : (s + 1) * 512, :].rearrange("(p j) i -> p j i", j=PACK)
+            if (e, s) == (E - 1, PASSES - 1):
+                nc.sync.dma_start(out=raw[:, :, : H // 2], in_=rows[:, :, : H // 2])
+                nc.sync.dma_start(out=raw[:, :, H // 2 :], in_=rows[:, :, H // 2 :])
+            else:
+                nc.sync.dma_start(out=raw[:], in_=rows)
             return raw
 
         def load_wat(e):
@@ -83,12 +88,10 @@ def tile_moe_adb_none_kernel(
             nc.sync.dma_start(out=raw[:], in_=wat[e].rearrange("(p j) k -> p j k", j=PACK))
             return raw
 
-        def cast_wbt(raw, half, split):
+        def cast_wbt(raw, half, m0, m1):
             dst = half.rearrange("p (t m j) -> p m j t", t=PACK, j=PACK)
             src = raw[:].rearrange("p j (m t) -> p m j t", t=PACK)
-            nc.scalar.copy(dst[:, :split], src[:, :split])
-            if split < P:
-                nc.vector.tensor_copy(dst[:, split:], src[:, split:])
+            nc.scalar.copy(dst[:, m0:m1], src[:, m0:m1])
 
         def cast_wat(raw, half, copy):
             copy(
@@ -105,19 +108,18 @@ def tile_moe_adb_none_kernel(
         def cols_of(mx, c0, c1):
             return mx[0][:, c0:c1].bitcast(FP8X4), mx[1][:, c0:c1]
 
-        def gather(e):
+        def gather(e, part, period=-1, at=0):
             idx = offs_sb[:, e * C // 16 : (e + 1) * C // 16]
-            words = []
-            for s in range(PASSES):
-                w = held([P, C], U32, "gw%d_%d" % (e, s), e - GATHER_LEAD, 1, s * C * 4)
-                nc.vector.tensor_copy(w[:], dyw[s][:].bitcast(U32).indirect(idx))
-                words.append(w)
-            z = held([P, C], U8, "gs%d" % e, e - GATHER_LEAD, 1, PASSES * C * 4)
-            nc.vector.tensor_copy(z[:], dys[:].indirect(idx))
-            return words, z
+            if part < PASSES:
+                window, dtype = dyw[part][:].bitcast(U32), U32
+            else:
+                window, dtype = dys[:], U8
+            picked = held([P, C], dtype, "picked%d_%d" % (e, part), period, 1, at)
+            nc.vector.tensor_copy(picked[:], window.indirect(idx))
+            g[e, part] = picked
 
-        def first_product(wq, g):
-            words, z = g
+        def first_product(wq, e):
+            words, z = [g[e, s] for s in range(PASSES)], g[e, PASSES]
             banks = []
             for h in range(C // P):
                 cols = slice(h * P, (h + 1) * P)
@@ -137,30 +139,33 @@ def tile_moe_adb_none_kernel(
                 banks.append(bank)
             return banks
 
-        def apply_gate(e, banks, dh):
-            for h, bank in enumerate(banks):
-                u, j0 = divmod(e * C + h * P, SLOTS // 2)
-                nc.vector.tensor_tensor(
-                    dh[:, h * P * PACK : (h + 1) * P * PACK].rearrange("p (n t) -> p n t", t=PACK),
-                    bank[:].rearrange("p t n -> p n t"),
-                    gate_sb[u][:, j0 : j0 + P].unsqueeze(2).to_broadcast([P, P, PACK]),
-                    MULT,
-                )
+        def apply_gate(e, h, banks, dh):
+            u, j0 = divmod(e * C + h * P, SLOTS // 2)
+            nc.vector.tensor_tensor(
+                dh[:, h * P * PACK : (h + 1) * P * PACK].rearrange("p (n t) -> p n t", t=PACK),
+                banks[h][:].rearrange("p t n -> p n t"),
+                gate_sb[u][:, j0 : j0 + P].unsqueeze(2).to_broadcast([P, P, PACK]),
+                MULT,
+            )
 
-        def second_product(e, aq, hq, copy):
+        def second_product(aq, hq, width=C):
             bank = ps_x.tile([P, KB, C], F32, name="bank")
-            h_codes, h_scales = cols_of(hq, 0, C)
-            for kb in range(KB):
-                a_codes, a_scales = cols_of(aq, C + kb * P, C + (kb + 1) * P)
-                nc.tensor.matmul_mx(
-                    out=bank[:, kb, :],
-                    lhsT=a_codes,
-                    lhsT_scale=a_scales,
-                    rhs=h_codes,
-                    rhs_scale=h_scales,
-                    start=True,
-                    stop=True,
-                )
+            for c0 in range(0, C, width):
+                h_codes, h_scales = cols_of(hq, c0, c0 + width)
+                for kb in range(KB):
+                    a_codes, a_scales = cols_of(aq, C + kb * P, C + (kb + 1) * P)
+                    nc.tensor.matmul_mx(
+                        out=bank[:, kb, c0 : c0 + width],
+                        lhsT=a_codes,
+                        lhsT_scale=a_scales,
+                        rhs=h_codes,
+                        rhs_scale=h_scales,
+                        start=True,
+                        stop=True,
+                    )
+            return bank
+
+        def keep_dx(e, bank, copy):
             for kb in range(KB):
                 copy(dx[kb][:, e * C : (e + 1) * C], bank[:, kb, :])
 
@@ -181,8 +186,8 @@ def tile_moe_adb_none_kernel(
                 base.append(bank)
             return base
 
-        def leave_psum(kb, bank, e):
-            part = held([P, T], F32, "base%d" % kb, e, 0, 0)
+        def leave_psum(kb, bank):
+            part = raw_b.tile([P, T], F32, name="base%d" % kb, offset=wat_offset(E - 1) + kb * T * 4, align_bytes=64)
             nc.scalar.copy(part[:], bank[:])
             return part
 
@@ -202,7 +207,7 @@ def tile_moe_adb_none_kernel(
                 held([P, C + K], U8, "pair_scales%d" % b, b + 1, 1, 6144),
             )
 
-        base = []
+        late = [(e, part) for e in range(GATHER_LEAD, E) for part in range(PASSES + 1)]
         for e in range(E):
             last = e == E - 1
             if e > 0:
@@ -222,54 +227,76 @@ def tile_moe_adb_none_kernel(
             if e == 3:
                 nc.sync.dma_start(gate_sb[1][:], gate[:, SLOTS // 2 :])
             if e == 0:
-                for first in range(GATHER_LEAD):
-                    g[first] = gather(first)
-            half = half_b.tile([P, PASSES * H * PACK], BF16, name="half", align_bytes=64)
+                for part in range(PASSES + 1):
+                    for first in range(GATHER_LEAD):
+                        gather(first, part)
+            b = e - 1
+            half_at = HALF_AT + e % HALF_SLOTS * PASSES * H * PACK * 2
+            half = raw_b.tile([P, PASSES * H * PACK], BF16, name="half%d" % e, offset=half_at, align_bytes=64)
             wq = (
                 code_b.tile([P, PASSES * H], U32, name="wb_codes", align_bytes=64),
                 code_b.tile([P, PASSES * H], U8, name="wb_scales", align_bytes=64),
             )
-            cast_wbt(rb[e, 0], half[:, : H * PACK], SPLIT if last else P)
-            if last:
+            early = e >= E - 2
+            cast_wbt(rb[e, 0], half[:, : H * PACK], 0, P)
+            if early:
                 quantize(wq, half, 0, H)
-            cast_wbt(rb[e, 1], half[:, H * PACK :], 48 if last else SPLIT if e >= GATHER_LEAD else P)
-            quantize(wq, half, H if last else 0, PASSES * H)
-            if e in (5, 6):
-                base.append(leave_psum(e - 5, base_banks[e - 5], e))
-            if e >= GATHER_LEAD:
-                pair[e] = held([P, (C + K) * PACK], BF16, "pair%d" % e, e, 1, 0)
-            else:
-                pair[e] = ring.tile([P, (C + K) * PACK], BF16, name="pair", align_bytes=64)
-            b = e - 1
             if last:
-                banks = first_product(wq, g[e])
-                apply_gate(e, banks, pair[e])
-                pair[E] = ring.tile([P, (C + K) * PACK], BF16, name="pair", align_bytes=64)
-                for a in range(E - TAIL_WAT, E):
-                    cast_wat(ra[a], pair[a + 1][:, C * PACK :], nc.scalar.copy)
+                cast_wbt(rb[e, 1], half[:, H * PACK :], 0, P // 2)
+                cast_wbt(rb[e, 1], half[:, H * PACK :], P // 2, P)
+                quantize(wq, half, H, H + H // 2)
+                quantize(wq, half, H + H // 2, PASSES * H)
+                banks = first_product(wq, e)
+            else:
+                cast_wbt(rb[e, 1], half[:, H * PACK :], 0, P)
             if b >= 0:
                 pair_mx[b] = new_pair_mx(b)
                 quantize(pair_mx[b], pair[b], 0, C + K if b > 0 else C)
             if b >= 1:
-                second_product(b - 1, pair_mx[b], pair_mx[b - 1], nc.vector.tensor_copy if not last else nc.scalar.copy)
+                dx_bank = second_product(pair_mx[b], pair_mx[b - 1])
             if not last:
-                banks = first_product(wq, g[e])
-                if e + GATHER_LEAD < E:
-                    g[e + GATHER_LEAD] = gather(e + GATHER_LEAD)
-                if 1 <= e <= E - TAIL_WAT:
-                    copy = nc.vector.tensor_copy if e >= GATHER_LEAD else nc.scalar.copy
-                    cast_wat(ra[e - 1], pair[e][:, C * PACK :], copy)
-                apply_gate(e, banks, pair[e])
+                quantize(wq, half, H if early else 0, PASSES * H)
+                banks = first_product(wq, e)
+            for u in range(min(1, LATE[e])):
+                gather(*late.pop(0), e, 0)
+            if b >= 1 and not last:
+                keep_dx(b - 1, dx_bank, nc.vector.tensor_copy)
+            if not last:
+                pair[e] = raw_b.tile([P, (C + K) * PACK], BF16, name="pair%d" % e, offset=half_at, align_bytes=64)
+            if last:
+                pair[e] = keep.tile([P, (C + K) * PACK], BF16, name="pair_e", align_bytes=64)
+                pair[E] = keep.tile([P, (C + K) * PACK], BF16, name="pair_last", align_bytes=64)
+                for a in range(E - TAIL_WAT, E):
+                    cast_wat(ra[a], pair[a + 1][:, C * PACK :], nc.scalar.copy)
+            elif e >= 1:
+                nc.gpsimd.tensor_scalar(
+                    pair[e][:, C * PACK :].rearrange("p (c j) -> p c j", j=PACK),
+                    ra[e - 1][:].rearrange("p j c -> p c j"),
+                    1.0,
+                    0.0,
+                    MULT,
+                    ADD,
+                )
+            apply_gate(e, 0, banks, pair[e])
+            if LATE[e] > 1:
+                gather(*late.pop(0), e, C * 4)
+            if last:
+                pair_mx[E - 1] = new_pair_mx(E - 1)
+                pair_mx[E] = new_pair_mx(E)
+                quantize(pair_mx[E - 1], pair[E - 1], C, C + K)
+                quantize(pair_mx[E], pair[E], C, C + K)
+                quantize(pair_mx[E - 1], pair[E - 1], 0, P)
+            apply_gate(e, 1, banks, pair[e])
+            if LATE[e] > 2:
+                gather(*late.pop(0), e, 2 * C * 4)
             if e == 2:
                 base_banks = frozen_layer()
 
-        pair_mx[E - 1] = new_pair_mx(E - 1)
-        pair_mx[E] = new_pair_mx(E)
-        quantize(pair_mx[E - 1], pair[E - 1], 0, C)
-        quantize(pair_mx[E - 1], pair[E - 1], C, C + K)
-        quantize(pair_mx[E], pair[E], C, C + K)
-        second_product(E - 2, pair_mx[E - 1], pair_mx[E - 2], nc.vector.tensor_copy)
-        second_product(E - 1, pair_mx[E], pair_mx[E - 1], nc.scalar.copy)
+        quantize(pair_mx[E - 1], pair[E - 1], P, C)
+        keep_dx(E - 3, dx_bank, nc.vector.tensor_copy)
+        base = [leave_psum(kb, base_banks[kb]) for kb in range(KB)]
+        keep_dx(E - 2, second_product(pair_mx[E - 1], pair_mx[E - 2]), nc.scalar.copy)
+        keep_dx(E - 1, second_product(pair_mx[E], pair_mx[E - 1], P), nc.scalar.copy)
 
         acc = base
         for r in range(TOP):

@@ -1,6 +1,7 @@
 from contextlib import ExitStack
 
 import concourse.mybir as mybir
+from concourse.masks import make_identity
 
 K, T, E, C, H, N, TOP = 256, 512, 8, 256, 512, 1024, 4
 FLOPS = 2 * N * K * T + 2 * E * C * H * (N + K)
@@ -47,7 +48,9 @@ def tile_moe_adb_none_kernel(
         dys = keep.tile([P, T], U8, name="dys", align_bytes=64)
         wtw = keep.tile([P, PASSES, K], I32, name="wtw", align_bytes=64)
         wts = keep.tile([P, K], U8, name="wts", align_bytes=64)
-        gate_sb = [keep.tile([P, SLOTS // 2], F32, name="gate_sb%d" % u) for u in range(2)]
+        gate_sb = [keep.tile([P, 4 * P], F32, name="gate_sb%d" % u) for u in range(SLOTS // (4 * P))]
+        ident = keep.tile([P, P], F32, name="ident")
+        make_identity(nc, ident[:])
         dx = [keep.tile([P, SLOTS], F32, name="dx%d" % kb) for kb in range(KB)]
 
         def load_words(dst, src):
@@ -140,7 +143,7 @@ def tile_moe_adb_none_kernel(
             return banks
 
         def apply_gate(e, h, banks, dh):
-            u, j0 = divmod(e * C + h * P, SLOTS // 2)
+            u, j0 = divmod(e * C + h * P, 4 * P)
             nc.vector.tensor_tensor(
                 dh[:, h * P * PACK : (h + 1) * P * PACK].rearrange("p (n t) -> p n t", t=PACK),
                 banks[h][:].rearrange("p t n -> p n t"),
@@ -196,10 +199,23 @@ def tile_moe_adb_none_kernel(
         nc.sync.dma_start(offs_sb[:], offs)
         load_words(dyw[0][:], dy_words[0])
         load_words(dyw[1][:], dy_words[1])
-        load_scales(dys, dy_scales)
+        gate_rows = keep.tile([P, P], F32, name="gate_rows")
+        nc.vector.memset(gate_rows[:], 0.0)
+        nc.sync.dma_start(out=gate_rows[: SLOTS // P, :], in_=gate[0].rearrange("(b n) -> b n", n=P))
         rb[0, 0] = load_wbt(0, 0)
+        load_scales(dys, dy_scales)
         rb[0, 1] = load_wbt(0, 1)
-        nc.sync.dma_start(gate_sb[0][:], gate[:, : SLOTS // 2])
+
+        turned = ps_x.tile([P, KB, C], F32, name="bank")
+        nc.tensor.transpose(turned[:, 0, :P], gate_rows[:], ident[:])
+        gate_cols = keep.tile([P, SLOTS // P], F32, name="gate_cols")
+        nc.scalar.copy(gate_cols[:], turned[:, 0, : SLOTS // P])
+        for part_no, part in enumerate(gate_sb):
+            bank = ps_h.tile([P, PACK, P], F32, name="bank")
+            for b in range(4):
+                col = gate_cols[:, 4 * part_no + b : 4 * part_no + b + 1]
+                nc.tensor.transpose(bank[:, b, :], col.to_broadcast([P, P]), ident[:])
+            nc.scalar.copy(part[:], bank[:].rearrange("p b n -> p (b n)"))
 
         def new_pair_mx(b):
             return (
@@ -211,8 +227,9 @@ def tile_moe_adb_none_kernel(
         for e in range(E):
             last = e == E - 1
             if e > 0:
-                rb[e, 0] = load_wbt(e, 0)
                 rb[e, 1] = load_wbt(e, 1)
+            if not last:
+                rb[e + 1, 0] = load_wbt(e + 1, 0)
             if 1 <= e <= E - TAIL_WAT:
                 ra[e - 1] = load_wat(e - 1)
             if last:
@@ -224,8 +241,6 @@ def tile_moe_adb_none_kernel(
             if e == 2:
                 load_scales(wts, wt_scales)
                 nc.sync.dma_start(out=wtw[:], in_=wt_words.rearrange("s p x d -> p s (x d)").bitcast(I32))
-            if e == 3:
-                nc.sync.dma_start(gate_sb[1][:], gate[:, SLOTS // 2 :])
             if e == 0:
                 for part in range(PASSES + 1):
                     for first in range(GATHER_LEAD):
@@ -260,7 +275,7 @@ def tile_moe_adb_none_kernel(
             for u in range(min(1, LATE[e])):
                 gather(*late.pop(0), e, 0)
             if b >= 1 and not last:
-                keep_dx(b - 1, dx_bank, nc.vector.tensor_copy)
+                keep_dx(b - 1, dx_bank, nc.scalar.copy if b % 2 == 1 else nc.vector.tensor_copy)
             if not last:
                 pair[e] = raw_b.tile([P, (C + K) * PACK], BF16, name="pair%d" % e, offset=half_at, align_bytes=64)
             if last:

from contextlib import ExitStack

import concourse.mybir as mybir
from concourse.masks import make_identity

K, T, E, C, H, N, TOP = 256, 512, 8, 256, 512, 1024, 4
FLOPS = 2 * N * K * T + 2 * E * C * H * (N + K)

F32 = mybir.dt.float32
BF16 = mybir.dt.bfloat16
I32 = mybir.dt.int32
U32 = mybir.dt.uint32
U16 = mybir.dt.uint16
U8 = mybir.dt.uint8
FP8X4 = mybir.dt.float8_e4m3fn_x4
ADD = mybir.AluOpType.add
MULT = mybir.AluOpType.mult

P = 128
PACK = 4
PASSES = N // (P * PACK)
KB = K // P
SLOTS = E * C
TAIL_WAT = 2
HALF_SLOTS = 3
LATE = (2, 2, 3, 3, 2, 0, 0, 0)
GATHER_LEAD = 4
RAW_SLOTS = 12
RAW_BYTES = PACK * H * 4
HALF_AT = RAW_SLOTS * RAW_BYTES + 4 * PACK * K * 4


def tile_moe_adb_none_kernel(
    tc, dy_words, dy_scales, wt_words, wt_scales, wbt, wat, gate, offs, pos1, pos2, pos3, pos4, out
):
    nc = tc.nc
    with ExitStack() as ctx:
        keep = ctx.enter_context(tc.tile_pool(name="keep", bufs=1))
        raw_b = ctx.enter_context(tc.tile_pool(name="raw_b", bufs=1))
        code_b = ctx.enter_context(tc.tile_pool(name="code_b", bufs=3))
        ps_h = ctx.enter_context(tc.psum_pool(name="ps_h", bufs=4))
        ps_x = ctx.enter_context(tc.psum_pool(name="ps_x", bufs=2))
        ps_b = ctx.enter_context(tc.psum_pool(name="ps_b", bufs=2))

        offs_sb = keep.tile([P, SLOTS // 16], U16, name="offs_sb")
        pos_sb = [keep.tile([P, T // 16], U16, name="pos_sb%d" % r) for r in range(TOP)]
        dyw = [keep.tile([P, T], I32, name="dyw%d" % s, align_bytes=64) for s in range(PASSES)]
        dys = keep.tile([P, T], U8, name="dys", align_bytes=64)
        wtw = keep.tile([P, PASSES, K], I32, name="wtw", align_bytes=64)
        wts = keep.tile([P, K], U8, name="wts", align_bytes=64)
        gate_sb = [keep.tile([P, 4 * P], F32, name="gate_sb%d" % u) for u in range(SLOTS // (4 * P))]
        ident = keep.tile([P, P], F32, name="ident")
        make_identity(nc, ident[:])
        dx = [keep.tile([P, SLOTS], F32, name="dx%d" % kb) for kb in range(KB)]

        def load_words(dst, src):
            nc.sync.dma_start(out=dst, in_=src.rearrange("p x d -> p (x d)").bitcast(I32))

        def load_scales(plane, src):
            nc.vector.memset(plane[:].bitcast(I32), 0)
            for q in range(4):
                nc.sync.dma_start(
                    out=plane[32 * q : 32 * q + 4 * PASSES, :].bitcast(I32),
                    in_=src[:, 4 * q : 4 * q + 4, :].bitcast(I32),
                )

        def raw_offset(e, s):
            chunk = PASSES * e + s
            return (chunk if chunk < RAW_SLOTS else PASSES * (chunk - RAW_SLOTS)) * RAW_BYTES

        def wat_offset(e):
            return RAW_SLOTS * RAW_BYTES + e % 4 * PACK * K * 4

        def held(shape, dtype, name, e, s, at):
            if 0 <= e < E:
                return raw_b.tile(shape, dtype, name=name, offset=raw_offset(e, s) + at, align_bytes=64)
            return keep.tile(shape, dtype, name=name, align_bytes=64)

        def load_wbt(e, s):
            raw = raw_b.tile([P, PACK, H], F32, name="raw%d_%d" % (e, s), offset=raw_offset(e, s), align_bytes=64)
            rows = wbt[e, s * 512 : (s + 1) * 512, :].rearrange("(p j) i -> p j i", j=PACK)
            if (e, s) == (E - 1, PASSES - 1):
                nc.sync.dma_start(out=raw[:, :, : H // 2], in_=rows[:, :, : H // 2])
                nc.sync.dma_start(out=raw[:, :, H // 2 :], in_=rows[:, :, H // 2 :])
            else:
                nc.sync.dma_start(out=raw[:], in_=rows)
            return raw

        def load_wat(e):
            raw = raw_b.tile([P, PACK, K], F32, name="raw_a%d" % e, offset=wat_offset(e), align_bytes=64)
            nc.sync.dma_start(out=raw[:], in_=wat[e].rearrange("(p j) k -> p j k", j=PACK))
            return raw

        def cast_wbt(raw, half, m0, m1):
            dst = half.rearrange("p (t m j) -> p m j t", t=PACK, j=PACK)
            src = raw[:].rearrange("p j (m t) -> p m j t", t=PACK)
            nc.scalar.copy(dst[:, m0:m1], src[:, m0:m1])

        def cast_wat(raw, half, copy):
            copy(
                half.rearrange("p (c i j) -> p c j i", i=4, j=PACK),
                raw[:].rearrange("p j (c i) -> p c j i", i=4),
            )

        def quantize(mx, half, c0, c1):
            codes, scales = mx
            nc.vector.quantize_mx(
                out=codes[:, c0:c1].bitcast(FP8X4), scales=scales[:, c0:c1], in_=half[:, c0 * PACK : c1 * PACK]
            )

        def cols_of(mx, c0, c1):
            return mx[0][:, c0:c1].bitcast(FP8X4), mx[1][:, c0:c1]

        def gather(e, part, period=-1, at=0):
            idx = offs_sb[:, e * C // 16 : (e + 1) * C // 16]
            if part < PASSES:
                window, dtype = dyw[part][:].bitcast(U32), U32
            else:
                window, dtype = dys[:], U8
            picked = held([P, C], dtype, "picked%d_%d" % (e, part), period, 1, at)
            nc.vector.tensor_copy(picked[:], window.indirect(idx))
            g[e, part] = picked

        def first_product(wq, e):
            words, z = [g[e, s] for s in range(PASSES)], g[e, PASSES]
            banks = []
            for h in range(C // P):
                cols = slice(h * P, (h + 1) * P)
                bank = ps_h.tile([P, PACK, P], F32, name="bank")
                for t in range(PACK):
                    for s in range(PASSES):
                        codes, scales = cols_of(wq, s * H + t * P, s * H + (t + 1) * P)
                        nc.tensor.matmul_mx(
                            out=bank[:, t, :],
                            lhsT=codes,
                            lhsT_scale=scales,
                            rhs=words[s][:, cols].bitcast(FP8X4),
                            rhs_scale=z[4 * s :, cols],
                            start=(s == 0),
                            stop=(s == PASSES - 1),
                        )
                banks.append(bank)
            return banks

        def apply_gate(e, h, banks, dh):
            u, j0 = divmod(e * C + h * P, 4 * P)
            nc.vector.tensor_tensor(
                dh[:, h * P * PACK : (h + 1) * P * PACK].rearrange("p (n t) -> p n t", t=PACK),
                banks[h][:].rearrange("p t n -> p n t"),
                gate_sb[u][:, j0 : j0 + P].unsqueeze(2).to_broadcast([P, P, PACK]),
                MULT,
            )

        def second_product(aq, hq, width=C):
            bank = ps_x.tile([P, KB, C], F32, name="bank")
            for c0 in range(0, C, width):
                h_codes, h_scales = cols_of(hq, c0, c0 + width)
                for kb in range(KB):
                    a_codes, a_scales = cols_of(aq, C + kb * P, C + (kb + 1) * P)
                    nc.tensor.matmul_mx(
                        out=bank[:, kb, c0 : c0 + width],
                        lhsT=a_codes,
                        lhsT_scale=a_scales,
                        rhs=h_codes,
                        rhs_scale=h_scales,
                        start=True,
                        stop=True,
                    )
            return bank

        def keep_dx(e, bank, copy):
            for kb in range(KB):
                copy(dx[kb][:, e * C : (e + 1) * C], bank[:, kb, :])

        def frozen_layer():
            base = []
            for kb in range(KB):
                bank = ps_b.tile([P, T], F32, name="bank")
                for s in range(PASSES):
                    nc.tensor.matmul_mx(
                        out=bank[:],
                        lhsT=wtw[:, s, kb * P : (kb + 1) * P].bitcast(FP8X4),
                        lhsT_scale=wts[4 * s :, kb * P : (kb + 1) * P],
                        rhs=dyw[s][:].bitcast(FP8X4),
                        rhs_scale=dys[4 * s :, :],
                        start=(s == 0),
                        stop=(s == PASSES - 1),
                    )
                base.append(bank)
            return base

        def leave_psum(kb, bank):
            part = raw_b.tile([P, T], F32, name="base%d" % kb, offset=wat_offset(E - 1) + kb * T * 4, align_bytes=64)
            nc.scalar.copy(part[:], bank[:])
            return part

        rb, ra, g, pair, pair_mx = {}, {}, {}, {}, {}

        nc.sync.dma_start(offs_sb[:], offs)
        load_words(dyw[0][:], dy_words[0])
        load_words(dyw[1][:], dy_words[1])
        gate_rows = keep.tile([P, P], F32, name="gate_rows")
        nc.vector.memset(gate_rows[:], 0.0)
        nc.sync.dma_start(out=gate_rows[: SLOTS // P, :], in_=gate[0].rearrange("(b n) -> b n", n=P))
        rb[0, 0] = load_wbt(0, 0)
        load_scales(dys, dy_scales)
        rb[0, 1] = load_wbt(0, 1)

        turned = ps_x.tile([P, KB, C], F32, name="bank")
        nc.tensor.transpose(turned[:, 0, :P], gate_rows[:], ident[:])
        gate_cols = keep.tile([P, SLOTS // P], F32, name="gate_cols")
        nc.scalar.copy(gate_cols[:], turned[:, 0, : SLOTS // P])
        for part_no, part in enumerate(gate_sb):
            bank = ps_h.tile([P, PACK, P], F32, name="bank")
            for b in range(4):
                col = gate_cols[:, 4 * part_no + b : 4 * part_no + b + 1]
                nc.tensor.transpose(bank[:, b, :], col.to_broadcast([P, P]), ident[:])
            nc.scalar.copy(part[:], bank[:].rearrange("p b n -> p (b n)"))

        def new_pair_mx(b):
            return (
                held([P, C + K], U32, "pair_codes%d" % b, b + 1, 1, 4096),
                held([P, C + K], U8, "pair_scales%d" % b, b + 1, 1, 6144),
            )

        late = [(e, part) for e in range(GATHER_LEAD, E) for part in range(PASSES + 1)]
        for e in range(E):
            last = e == E - 1
            if e > 0:
                rb[e, 1] = load_wbt(e, 1)
            if not last:
                rb[e + 1, 0] = load_wbt(e + 1, 0)
            if 1 <= e <= E - TAIL_WAT:
                ra[e - 1] = load_wat(e - 1)
            if last:
                for a in range(E - TAIL_WAT, E):
                    ra[a] = load_wat(a)
            if e == 1:
                for r, pos in enumerate((pos1, pos2, pos3, pos4)):
                    nc.sync.dma_start(pos_sb[r][:], pos)
            if e == 2:
                load_scales(wts, wt_scales)
                nc.sync.dma_start(out=wtw[:], in_=wt_words.rearrange("s p x d -> p s (x d)").bitcast(I32))
            if e == 0:
                for part in range(PASSES + 1):
                    for first in range(GATHER_LEAD):
                        gather(first, part)
            b = e - 1
            half_at = HALF_AT + e % HALF_SLOTS * PASSES * H * PACK * 2
            half = raw_b.tile([P, PASSES * H * PACK], BF16, name="half%d" % e, offset=half_at, align_bytes=64)
            wq = (
                code_b.tile([P, PASSES * H], U32, name="wb_codes", align_bytes=64),
                code_b.tile([P, PASSES * H], U8, name="wb_scales", align_bytes=64),
            )
            early = e >= E - 2
            cast_wbt(rb[e, 0], half[:, : H * PACK], 0, P)
            if early:
                quantize(wq, half, 0, H)
            if last:
                cast_wbt(rb[e, 1], half[:, H * PACK :], 0, P // 2)
                cast_wbt(rb[e, 1], half[:, H * PACK :], P // 2, P)
                quantize(wq, half, H, H + H // 2)
                quantize(wq, half, H + H // 2, PASSES * H)
                banks = first_product(wq, e)
            else:
                cast_wbt(rb[e, 1], half[:, H * PACK :], 0, P)
            if b >= 0:
                pair_mx[b] = new_pair_mx(b)
                quantize(pair_mx[b], pair[b], 0, C + K if b > 0 else C)
            if b >= 1:
                dx_bank = second_product(pair_mx[b], pair_mx[b - 1])
            if not last:
                quantize(wq, half, H if early else 0, PASSES * H)
                banks = first_product(wq, e)
            for u in range(min(1, LATE[e])):
                gather(*late.pop(0), e, 0)
            if b >= 1 and not last:
                keep_dx(b - 1, dx_bank, nc.scalar.copy if b % 2 == 1 else nc.vector.tensor_copy)
            if not last:
                pair[e] = raw_b.tile([P, (C + K) * PACK], BF16, name="pair%d" % e, offset=half_at, align_bytes=64)
            if last:
                pair[e] = keep.tile([P, (C + K) * PACK], BF16, name="pair_e", align_bytes=64)
                pair[E] = keep.tile([P, (C + K) * PACK], BF16, name="pair_last", align_bytes=64)
                for a in range(E - TAIL_WAT, E):
                    cast_wat(ra[a], pair[a + 1][:, C * PACK :], nc.scalar.copy)
            elif e >= 1:
                nc.gpsimd.tensor_scalar(
                    pair[e][:, C * PACK :].rearrange("p (c j) -> p c j", j=PACK),
                    ra[e - 1][:].rearrange("p j c -> p c j"),
                    1.0,
                    0.0,
                    MULT,
                    ADD,
                )
            apply_gate(e, 0, banks, pair[e])
            if LATE[e] > 1:
                gather(*late.pop(0), e, C * 4)
            if last:
                pair_mx[E - 1] = new_pair_mx(E - 1)
                pair_mx[E] = new_pair_mx(E)
                quantize(pair_mx[E - 1], pair[E - 1], C, C + K)
                quantize(pair_mx[E], pair[E], C, C + K)
                quantize(pair_mx[E - 1], pair[E - 1], 0, P)
            apply_gate(e, 1, banks, pair[e])
            if LATE[e] > 2:
                gather(*late.pop(0), e, 2 * C * 4)
            if e == 2:
                base_banks = frozen_layer()

        quantize(pair_mx[E - 1], pair[E - 1], P, C)
        keep_dx(E - 3, dx_bank, nc.vector.tensor_copy)
        base = [leave_psum(kb, base_banks[kb]) for kb in range(KB)]
        keep_dx(E - 2, second_product(pair_mx[E - 1], pair_mx[E - 2]), nc.scalar.copy)
        keep_dx(E - 1, second_product(pair_mx[E], pair_mx[E - 1], P), nc.scalar.copy)

        acc = base
        for r in range(TOP):
            for kb in range(KB):
                nxt = keep.tile([P, T], F32, name="acc%d_%d" % (r, kb))
                nc.vector.tensor_tensor(nxt[:], dx[kb][:].indirect(pos_sb[r][:]), acc[kb][:], ADD)
                acc[kb] = nxt
        for kb in range(KB):
            nc.sync.dma_start(out=out[kb * P : (kb + 1) * P, :], in_=acc[kb][:])
